import numpy as np
import ml_dtypes


def mxq(x, axis, fmt="e4m3"):
    dtype, down = {"e4m3": (ml_dtypes.float8_e4m3fn, 7), "e5m2": (ml_dtypes.float8_e5m2, 14)}[fmt]
    v = np.moveaxis(np.asarray(x, np.float32).astype(ml_dtypes.bfloat16).astype(np.float64), axis, -1)
    blocks = v.reshape(v.shape[:-1] + (-1, 32))
    amax = np.abs(blocks).max(-1, keepdims=True)
    byte = np.maximum(np.where(amax > 0, np.frexp(amax)[1] - 1 + 127, 0) - down, 1)
    scale = np.exp2(byte - 127.0)
    codes = (blocks / scale).astype(np.float32).astype(dtype).astype(np.float64)
    return np.moveaxis((codes * scale).reshape(v.shape), -1, axis)


WIDE = False


def mx_kscale(k):
    if not WIDE:
        return np.ones(k)
    levels = np.array([10, -10, 5, -5, 0])
    if k % 512:
        return np.exp2(np.random.permutation(np.resize(levels, k // 32))).repeat(32)
    a = np.empty((k // 512, 16))
    for p in range(k // 512):
        a[p, :8] = np.random.permutation(np.resize(levels, 8))
        for g in range(8):
            far = levels[np.abs(levels - a[p, g]) >= 10]
            a[p, g + 8] = far[np.random.randint(len(far))]
    return np.exp2(a.ravel()).repeat(32)


def f64(x):
    return np.asarray(x).astype(np.float64)


def striped(idx):
    return np.tile(idx.reshape(-1, 16).T, (8, 1)).astype(np.uint16)


def unstriped(offs):
    return offs[:16].T.reshape(-1).astype(np.int64)


def striped8(idx):
    return np.concatenate([x.reshape(-1, 16).T for x in idx]).astype(np.uint16)


def runs(offs, k):
    lists = np.stack([offs[16 * r : 16 * r + 16].T.reshape(-1) for r in range(8)]).astype(np.int64)
    return lists[np.arange(k) % 512 // 64]


def pack_weight(w):
    k, n = w.shape
    w = f64(np.asarray(w, np.float32).astype(ml_dtypes.bfloat16)).reshape(k // 32, 32, n)
    amax = np.abs(w).max(1)
    byte = np.clip(np.where(amax > 0, np.frexp(amax)[1] - 1 + 127 - 7, 1), 1, 254)
    scaled = (w * np.exp2(127.0 - byte)[:, None, :]).reshape(k, n).astype(np.float32)
    words = np.ascontiguousarray(scaled.reshape(k // 512, 128, 4, n).transpose(0, 1, 3, 2)).astype(ml_dtypes.float8_e4m3fn).view(np.uint8)
    return words, np.ascontiguousarray(byte.astype(np.uint8).reshape(k // 512, 16, n))


def unpack_weight(words, scales):
    g, p, n, _ = words.shape
    vals = np.ascontiguousarray(words).view(ml_dtypes.float8_e4m3fn).astype(np.float64) * np.repeat(np.exp2(scales.astype(np.float64) - 127.0), 8, axis=1)[..., None]
    return vals.transpose(0, 1, 3, 2).reshape(g * 512, n)


def sigmoid(v):
    return 1.0 / (1.0 + np.exp(-np.maximum(v, -700.0)))


K, T, S, N, G, H, W = 512, 1024, 512, 512, 2048, 512, 256


def setup_inputs():
    n = np.random.standard_normal
    s = mx_kscale(K)[:, None]
    u = mx_kscale(S)
    packed_xT = pack_weight(n((K, T)) * s)
    packed_dT = pack_weight(n((K, G)) / s)
    perm = np.stack([np.random.permutation(S) for _ in range(8)])
    perm2 = np.random.permutation(S)
    return {
        "x_words": packed_xT[0],
        "x_scales": packed_xT[1],
        "d_words": packed_dT[0],
        "d_scales": packed_dT[1],
        "gn": (np.random.uniform(0.5, 1.5, (H, 1)) * u[:, None]).astype(np.float32),
        "gm": (np.random.uniform(0.5, 1.5, (H, 1)) * u[:, None]).astype(np.float32),
        "w1": (n((H, N)) / np.sqrt(2 * H) / u[:, None]).astype(np.float32),
        "w2": (n((H, N)) / np.sqrt(2 * H) / u[:, None]).astype(np.float32),
        "offs": striped(np.random.permutation(T)[:S]),
        "k1": striped8(np.random.randint(0, G, (8, H))),
        "two": striped(np.random.permutation(T)[:S]),
        "n1": striped8(perm[:, :W]),
        "n2": striped8(perm[:, W:]),
        "n3": striped(perm2[:W]),
        "n4": striped(perm2[W:]),
        "n5": striped(np.random.randint(0, S, G)),
    }


def reference(x_words, x_scales, d_words, d_scales, gn, gm, w1, w2, offs, k1, two, n1, n2, n3, n4, n5):
    d_k1 = unpack_weight(d_words, d_scales)[np.arange(K)[:, None], runs(k1, K)]
    xq = unpack_weight(x_words, x_scales)[:, unstriped(offs)]
    a = 0.0625 * (d_k1.T @ xq)
    pa = a[np.arange(H)[:, None], runs(n1, H)]
    pb = a[np.arange(H)[:, None], runs(n2, H)]
    rb = pa * pb
    ra = pa + pb
    ds = np.zeros((H, S))
    ds[np.arange(H)[:, None], runs(n1, H)] = ra
    dt = ds.copy()
    dt[np.arange(H)[:, None], runs(n2, H)] = rb
    z = f64(gn) * dt
    x_two = unpack_weight(x_words, x_scales)[:, unstriped(two)]
    b = 0.0625 * (d_k1.T @ x_two)
    pb2 = b[:, unstriped(n4)]
    pa2 = b[:, unstriped(n3)]
    rb2 = pb2 * sigmoid(pb2 - pa2)
    ra2 = pa2 * sigmoid(pa2 - pb2)
    ds2 = np.zeros((H, S))
    ds2[:, unstriped(n3)] = ra2
    dt2 = ds2.copy()
    dt2[:, unstriped(n4)] = rb2
    z2 = f64(gm) * dt2
    h = mxq(f64(w1), 0, "e4m3").T @ mxq(z, 0, "e4m3") + mxq(f64(w2), 0, "e4m3").T @ mxq(z2, 0, "e4m3")
    mb = h[:, unstriped(n5)]
    mn = mb.reshape(N, S, 4).min(axis=2)
    mx = mb.reshape(N, S, 4).max(axis=2)
    return np.maximum(h, mn) - (0.5 * mx)

@@ -1,0 +1,287 @@
+from contextlib import ExitStack
+
+import concourse.mybir as mybir
+
+F32 = mybir.dt.float32
+BF16 = mybir.dt.bfloat16
+I32 = mybir.dt.int32
+U32 = mybir.dt.uint32
+U16 = mybir.dt.uint16
+U8 = mybir.dt.uint8
+FP8X4 = mybir.dt.float8_e4m3fn_x4
+ALU = mybir.AluOpType
+ACT = mybir.ActivationFunctionType
+
+P = 128
+PACK = 4
+T, G, S, W = 1024, 2048, 512, 256
+SPARE = 16
+PIECE = 512
+SPLIT = 352
+FLOPS = 4 * 2 * 512 * 512 * 512
+
+
+def tile_picked_kjbondduelgmid_none_p_kernel(
+    tc, x_words, x_scales, d_words, d_scales, gn, gm, w1, w2, offs, k1, two, n1, n2, n3, n4, n5, out
+):
+    nc = tc.nc
+    with ExitStack() as ctx:
+        lists = ctx.enter_context(tc.tile_pool(name="lists", bufs=1))
+        keep = ctx.enter_context(tc.tile_pool(name="keep", bufs=1))
+        ring = ctx.enter_context(tc.tile_pool(name="ring", bufs=4))
+        psum = ctx.enter_context(tc.psum_pool(name="psum", bufs=1))
+
+        def load_list(src, name):
+            tile = lists.tile(list(src.shape), U16, name=name)
+            nc.sync.dma_start(tile[:], src)
+            return tile
+
+        d_bytes = keep.tile([P, G], U8, name="d_bytes", align_bytes=64)
+        x_bytes = keep.tile([P, T], U8, name="x_bytes", align_bytes=64)
+        nc.gpsimd.memset(d_bytes[:].bitcast(I32), 0)
+        nc.vector.memset(x_bytes[:].bitcast(I32), 0)
+
+        x_tab = keep.tile([P, T], U32, name="x_tab", align_bytes=64)
+        nc.sync.dma_start(x_tab[:].bitcast(I32), x_words[0].rearrange("p n t -> p (n t)").bitcast(I32))
+        d_rows = d_scales[0].bitcast(I32).rearrange("(r e) n -> e r n", e=2)
+        for e in range(2):
+            nc.sync.dma_start(d_bytes[:].bitcast(I32)[e:P:16, :], d_rows[e])
+        k1_sb = load_list(k1, "k1_sb")
+        two_sb = load_list(two, "two_sb")
+        d_tab = keep.tile([P, G], U32, name="d_tab", tag="d_tab_then_w2", align_bytes=64)
+        nc.sync.dma_start(d_tab[:].bitcast(I32), d_words[0].rearrange("p n t -> p (n t)").bitcast(I32))
+        x_rows = x_scales[0].bitcast(I32)
+        for q in range(4):
+            nc.sync.dma_start(x_bytes[:].bitcast(I32)[32 * q : 32 * q + 4, :], x_rows[4 * q : 4 * q + 4, :])
+        w1_halves = []
+        for half in range(2):
+            raw = keep.tile([P, PACK, W], F32, name="w1_raw%d" % half)
+            nc.sync.dma_start(raw[:], w1.rearrange("(p t) m -> p t m", t=PACK)[:, :, W * half : W * (half + 1)])
+            w1_halves.append(raw)
+        offs_sb = load_list(offs, "offs_sb")
+        n3_sb = load_list(n3, "n3_sb")
+        n4_sb = load_list(n4, "n4_sb")
+        n1_sb = load_list(n1, "n1_sb")
+        n2_sb = load_list(n2, "n2_sb")
+        n5_sb = load_list(n5, "n5_sb")
+        gn_sb = keep.tile([P, PACK], F32, name="gn_sb")
+        gm_sb = keep.tile([P, PACK], F32, name="gm_sb")
+        nc.gpsimd.dma_start(gn_sb[:], gn.rearrange("(p t) o -> p (t o)", t=PACK))
+        nc.gpsimd.dma_start(gm_sb[:], gm.rearrange("(p t) o -> p (t o)", t=PACK))
+
+        key_bytes_list = keep.tile([P, S], U8, name="key_bytes_list", align_bytes=64)
+        nc.vector.tensor_copy(key_bytes_list[:], d_bytes[:].indirect(k1_sb[:]))
+        key_bytes = keep.tile([P, S], U8, name="key_bytes", align_bytes=64)
+        nc.vector.tensor_copy(
+            key_bytes[:].rearrange("p (t m) -> p t m", t=PACK),
+            key_bytes_list[:].rearrange("p (m t) -> p t m", t=PACK),
+        )
+        for e in range(2):
+            nc.scalar.dma_start(key_bytes[:].bitcast(I32)[2 + e : P : 32, :], key_bytes[:].bitcast(I32)[16 + e : P : 32, :])
+
+        def pick_words(list_sb, name, slot):
+            words = keep.tile([P, S], U32, name=name, tag=slot, align_bytes=64)
+            nc.vector.tensor_copy(words[:], x_tab[:].indirect(list_sb[:]))
+            return words
+
+        def pick_bytes(list_sb, name):
+            picked = keep.tile([P, S], U8, name=name, align_bytes=64)
+            nc.vector.tensor_copy(picked[:], x_bytes[:].indirect(list_sb[:]))
+            return picked
+
+        b_words = pick_words(two_sb, "b_words", "b_words")
+        key_words_list = keep.tile([P, S], U32, name="key_words_list", tag="key_then_a_words", align_bytes=64)
+        nc.vector.tensor_copy(key_words_list[:], d_tab[:].indirect(k1_sb[:]))
+        key_words = keep.tile([P, S], U32, name="key_words", align_bytes=64)
+        nc.vector.tensor_copy(
+            key_words[:].rearrange("p (t m) -> p t m", t=PACK),
+            key_words_list[:].rearrange("p (m t) -> p t m", t=PACK),
+        )
+        w2_raw = keep.tile([P, PACK, S], F32, name="w2_raw", tag="d_tab_then_w2", align_bytes=64)
+        nc.sync.dma_start(w2_raw[:], w2.rearrange("(p t) m -> p t m", t=PACK))
+        w1_woven = keep.tile([P, S, PACK], BF16, name="w1_woven", align_bytes=64)
+        for half in range(2):
+            nc.scalar.copy(w1_woven[:, W * half : W * (half + 1), :], w1_halves[half][:].rearrange("p t c -> p c t"))
+        b_bytes = pick_bytes(two_sb, "b_bytes")
+        a_words = pick_words(offs_sb, "a_words", "key_then_a_words")
+        a_bytes = pick_bytes(offs_sb, "a_bytes")
+
+        def score(words, scale_bytes, t, tag):
+            cols = slice(P * t, P * (t + 1))
+            bank = psum.tile([P, S], F32, name=tag)
+            nc.tensor.matmul_mx(
+                out=bank[:],
+                lhsT=key_words[:, cols].bitcast(FP8X4),
+                lhsT_scale=key_bytes[:, cols],
+                rhs=words[:].bitcast(FP8X4),
+                rhs_scale=scale_bytes[:],
+                start=True,
+                stop=True,
+            )
+            return bank
+
+        b_banks = [score(b_words, b_bytes, t, "bank%d" % t) for t in range(PACK)]
+        a_banks = [score(a_words, a_bytes, t, "bank%d" % (PACK + t)) for t in range(PACK)]
+
+        def weave(planes, name):
+            woven = keep.tile([P, S, PACK], BF16, name=name + "_woven", align_bytes=64)
+            nc.vector.tensor_copy(woven[:], planes[:].rearrange("p t c -> p c t"))
+            return woven
+
+        def quantise(woven, name):
+            words = keep.tile([P, S], U32, name=name + "_words", align_bytes=64)
+            scale_bytes = keep.tile([P, S], U8, name=name + "_bytes", align_bytes=64)
+            nc.vector.quantize_mx(out=words[:].bitcast(FP8X4), scales=scale_bytes[:], in_=woven[:].rearrange("p c t -> p (c t)"))
+            return words, scale_bytes
+
+        z_planes = keep.tile([P, PACK, S], BF16, name="z_planes", align_bytes=64)
+        z2_planes = keep.tile([P, PACK, S], BF16, name="z2_planes", align_bytes=64)
+
+        def row_tile(name, slot):
+            return keep.tile([P, S], F32, name=name, tag=slot)
+
+        def fetch(bank, first, second, name, slot):
+            row = row_tile(name + "_row", slot)
+            nc.scalar.activation(row[:], bank[:], ACT.Copy, scale=0.0625)
+            pair = ring.tile([P, 2 * W], F32, name=name + "_pair")
+            nc.scalar.activation(pair[:, :W], row[:].indirect(first[:]), ACT.Copy)
+            nc.scalar.activation(pair[:, W:], row[:].indirect(second[:]), ACT.Copy)
+            return pair
+
+        def fetch_a(t, slot):
+            return fetch(a_banks[t], n1_sb, n2_sb, "a", slot)
+
+        def fetch_b(t, slot):
+            pair = fetch(b_banks[t], n3_sb, n4_sb, "b", slot)
+            diff = ring.tile([P, W], F32, name="diff")
+            nc.vector.tensor_tensor(diff[:], pair[:, :W], pair[:, W:], ALU.subtract)
+            return pair, diff
+
+        def bond(pair, t):
+            placed = ring.tile([P, S], F32, name="a_placed")
+            nc.vector.tensor_tensor(placed[:].indirect(n1_sb[:]), pair[:, :W], pair[:, W:], ALU.add)
+            nc.vector.tensor_tensor(placed[:].indirect(n2_sb[:]), pair[:, :W], pair[:, W:], ALU.mult)
+            nc.vector.tensor_scalar(z_planes[:, t, :], placed[:], gn_sb[:, t : t + 1], None, ALU.mult)
+
+        def gates(diff, slot):
+            gate = row_tile("gate", slot)
+            nc.scalar.activation(gate[:, :W], diff[:], ACT.Sigmoid)
+            nc.scalar.activation(gate[:, W:], diff[:], ACT.Sigmoid, scale=-1.0)
+            return gate
+
+        def gate_product(pair, gate, slot):
+            gated = row_tile("gated", slot)
+            nc.vector.tensor_tensor(gated[:], pair[:], gate[:], ALU.mult)
+            return gated
+
+        def place_b_scalar(gated, t, slot):
+            placed = row_tile("b_placed", slot)
+            nc.scalar.activation(placed[:].indirect(n3_sb[:]), gated[:, :W], ACT.Copy)
+            nc.scalar.activation(placed[:].indirect(n4_sb[:]), gated[:, W:], ACT.Copy)
+            nc.scalar.activation(z2_planes[:, t, :], placed[:], ACT.Copy, scale=gm_sb[:, t : t + 1])
+
+        def place_b_vector(pair, gate, t, slot):
+            placed = row_tile("b_placed", slot)
+            nc.vector.tensor_tensor(placed[:].indirect(n3_sb[:]), pair[:, :W], gate[:, :W], ALU.mult)
+            nc.vector.tensor_tensor(placed[:].indirect(n4_sb[:]), pair[:, W:], gate[:, W:], ALU.mult)
+            nc.vector.tensor_scalar(z2_planes[:, t, :], placed[:], gm_sb[:, t : t + 1], None, ALU.mult)
+
+        b0, diff0 = fetch_b(0, "slot0")
+        w1_q = quantise(w1_woven, "w1")
+        w2_q = quantise(weave(w2_raw, "w2"), "w2")
+        b1, diff1 = fetch_b(1, "slot1")
+        a0 = fetch_a(0, "slot0")
+        gate0 = gates(diff0, "slot1")
+        gate1 = gates(diff1, "slot0")
+        bond(a0, 0)
+        gated0 = gate_product(b0, gate0, "slot2")
+        gated1 = gate_product(b1, gate1, "slot3")
+        bond(fetch_a(1, "slot4"), 1)
+        b2, diff2 = fetch_b(2, "slot5")
+        bond(fetch_a(2, "slot6"), 2)
+        b3, diff3 = fetch_b(3, "slot7")
+        a3 = fetch_a(3, "slot8")
+        gate2 = gates(diff2, "slot8")
+        gated2 = gate_product(b2, gate2, "slot9")
+        bond(a3, 3)
+        place_b_scalar(gated0, 0, "slot7")
+        gate3 = gates(diff3, "slot2")
+        z_q = quantise(weave(z_planes, "z"), "z")
+        place_b_vector(b3, gate3, 3, "slot10")
+        place_b_scalar(gated1, 1, "slot7")
+        place_b_scalar(gated2, 2, "slot7")
+        z2_woven = keep.tile([P, S, PACK], BF16, name="z2_woven", align_bytes=64)
+        nc.vector.tensor_copy(z2_woven[:, :SPLIT, :], z2_planes[:, :, :SPLIT].rearrange("p t c -> p c t"))
+        nc.scalar.copy(z2_woven[:, SPLIT:, :], z2_planes[:, :, SPLIT:].rearrange("p t c -> p c t"))
+        z2_q = quantise(z2_woven, "z2")
+
+        h_banks = []
+        for t in range(PACK):
+            cols = slice(P * t, P * (t + 1))
+            bank = psum.tile([P, S], F32, name="bank%d" % t)
+            for step, (w_q, v_q) in enumerate(((w1_q, z_q), (w2_q, z2_q))):
+                nc.tensor.matmul_mx(
+                    out=bank[:],
+                    lhsT=w_q[0][:, cols].bitcast(FP8X4),
+                    lhsT_scale=w_q[1][:, cols],
+                    rhs=v_q[0][:].bitcast(FP8X4),
+                    rhs_scale=v_q[1][:],
+                    start=(step == 0),
+                    stop=(step == 1),
+                )
+            h_banks.append(bank)
+
+        h_rows = []
+        for t in range(PACK):
+            h = keep.tile([P, S + SPARE], F32, name="h%d" % t)
+            nc.gpsimd.memset(h[:, S:], 0.0)
+            if t == 0:
+                nc.scalar.copy(h[:, :S], h_banks[t][:])
+            else:
+                nc.vector.tensor_copy(h[:, :S], h_banks[t][:])
+            h_rows.append(h)
+
+        def finish_top(piece):
+            h, result, start, stop, mn, mx, rows = piece
+            top = ring.tile([P, stop - start], F32, name="top")
+            nc.vector.tensor_tensor(top[:], h[:, start:stop], mn[:], ALU.max)
+            return top
+
+        def finish_out(piece, top):
+            h, result, start, stop, mn, mx, rows = piece
+            nc.vector.scalar_tensor_tensor(result[:, start:stop], mx[:], -0.5, top[:], ALU.mult, ALU.add)
+            nc.sync.dma_start(out[rows, start:stop], result[:, start:stop])
+
+        previous = None
+        for t in range(PACK):
+            result = ring.tile([P, S], F32, name="result")
+            members = ring.tile([P, S, PACK], F32, name="members")
+            flat = members[:].rearrange("p j t -> p (j t)")
+            for u in range(G // PIECE):
+                nc.scalar.activation(
+                    flat[:, PIECE * u : PIECE * (u + 1)],
+                    h_rows[t][:].indirect(n5_sb[:, u * PIECE // 16 : (u + 1) * PIECE // 16]),
+                    ACT.Copy,
+                )
+            if t == 0:
+                cuts = [0, 128, 256, 512]
+            elif t == PACK - 1:
+                cuts = [0, 256, 384, 512]
+            else:
+                cuts = [0, 256, 512]
+            for start, stop in zip(cuts, cuts[1:]):
+                groups = stop - start
+                low = ring.tile([P, groups, 2], F32, name="low")
+                high = ring.tile([P, groups, 2], F32, name="high")
+                mn = ring.tile([P, groups], F32, name="mn")
+                mx = ring.tile([P, groups], F32, name="mx")
+                nc.vector.tensor_tensor(low[:], members[:, start:stop, 0:2], members[:, start:stop, 2:4], ALU.min)
+                nc.vector.tensor_tensor(high[:], members[:, start:stop, 0:2], members[:, start:stop, 2:4], ALU.max)
+                if previous is not None:
+                    top = finish_top(previous)
+                nc.vector.tensor_tensor(mn[:], low[:, :, 0], low[:, :, 1], ALU.min)
+                if previous is not None:
+                    finish_out(previous, top)
+                nc.vector.tensor_tensor(mx[:], high[:, :, 0], high[:, :, 1], ALU.max)
+                previous = (h_rows[t], result, start, stop, mn, mx, slice(P * t, P * (t + 1)))
+        finish_out(previous, finish_top(previous))

@@ -36,28 +36,31 @@ def tile_picked_kjbondduelgmid_none_p_kernel(
             nc.sync.dma_start(tile[:], src)
             return tile
 
+        def weave_into(copy, woven, planes):
+            copy(woven.rearrange("p (c i) t -> p c t i", i=4), planes.rearrange("p t (c i) -> p c t i", i=4))
+
+        h_rows = [keep.tile([P, S + SPARE], F32, name="h%d" % t) for t in range(PACK)]
         d_bytes = keep.tile([P, G], U8, name="d_bytes", align_bytes=64)
         x_bytes = keep.tile([P, T], U8, name="x_bytes", align_bytes=64)
-        nc.gpsimd.memset(d_bytes[:].bitcast(I32), 0)
-        nc.vector.memset(x_bytes[:].bitcast(I32), 0)
+        key_bytes = keep.tile([P, S], U8, name="key_bytes", align_bytes=64)
 
-        x_tab = keep.tile([P, T], U32, name="x_tab", align_bytes=64)
-        nc.sync.dma_start(x_tab[:].bitcast(I32), x_words[0].rearrange("p n t -> p (n t)").bitcast(I32))
+        k1_sb = load_list(k1, "k1_sb")
         d_rows = d_scales[0].bitcast(I32).rearrange("(r e) n -> e r n", e=2)
         for e in range(2):
-            nc.sync.dma_start(d_bytes[:].bitcast(I32)[e:P:16, :], d_rows[e])
-        k1_sb = load_list(k1, "k1_sb")
-        two_sb = load_list(two, "two_sb")
+            nc.sync.dma_start(d_bytes[:].bitcast(I32)[e:P:2, :], d_rows[e].unsqueeze(1).broadcast_to([8, 8, G // 4]))
         d_tab = keep.tile([P, G], U32, name="d_tab", tag="d_tab_then_w2", align_bytes=64)
         nc.sync.dma_start(d_tab[:].bitcast(I32), d_words[0].rearrange("p n t -> p (n t)").bitcast(I32))
-        x_rows = x_scales[0].bitcast(I32)
-        for q in range(4):
-            nc.sync.dma_start(x_bytes[:].bitcast(I32)[32 * q : 32 * q + 4, :], x_rows[4 * q : 4 * q + 4, :])
-        w1_halves = []
-        for half in range(2):
-            raw = keep.tile([P, PACK, W], F32, name="w1_raw%d" % half)
-            nc.sync.dma_start(raw[:], w1.rearrange("(p t) m -> p t m", t=PACK)[:, :, W * half : W * (half + 1)])
-            w1_halves.append(raw)
+        two_sb = load_list(two, "two_sb")
+        x_rows = x_scales[0].bitcast(I32).rearrange("(q c) n -> c q n", c=4)
+        for c, queue in enumerate((nc.sync, nc.gpsimd, nc.gpsimd, nc.gpsimd)):
+            queue.dma_start(x_bytes[:].bitcast(I32)[c:P:4, :], x_rows[c].unsqueeze(1).broadcast_to([4, 8, T // 4]))
+        x_tab = keep.tile([P, T], U32, name="x_tab", align_bytes=64)
+        nc.sync.dma_start(x_tab[:].bitcast(I32), x_words[0].rearrange("p n t -> p (n t)").bitcast(I32))
+        nc.vector.memset(key_bytes[:].bitcast(I32), 0)
+        for h in h_rows:
+            nc.vector.memset(h[:, S:], 0.0)
+        warm = keep.tile([P, 1], F32, name="warm")
+        nc.scalar.activation(warm[:], h_rows[0][:, S : S + 1], ACT.Sigmoid)
         offs_sb = load_list(offs, "offs_sb")
         n3_sb = load_list(n3, "n3_sb")
         n4_sb = load_list(n4, "n4_sb")
@@ -71,13 +74,12 @@ def tile_picked_kjbondduelgmid_none_p_kernel(
 
         key_bytes_list = keep.tile([P, S], U8, name="key_bytes_list", align_bytes=64)
         nc.vector.tensor_copy(key_bytes_list[:], d_bytes[:].indirect(k1_sb[:]))
-        key_bytes = keep.tile([P, S], U8, name="key_bytes", align_bytes=64)
+        key_bytes_dealt = keep.tile([P, S], U8, name="key_bytes_dealt", tag="dealt_then_a_words", align_bytes=64)
         nc.vector.tensor_copy(
-            key_bytes[:].rearrange("p (t m) -> p t m", t=PACK),
-            key_bytes_list[:].rearrange("p (m t) -> p t m", t=PACK),
+            key_bytes_dealt[:].rearrange("p (t c i) -> p c t i", t=PACK, i=16),
+            key_bytes_list[:].rearrange("p (c i t) -> p c t i", t=PACK, i=16),
         )
-        for e in range(2):
-            nc.scalar.dma_start(key_bytes[:].bitcast(I32)[2 + e : P : 32, :], key_bytes[:].bitcast(I32)[16 + e : P : 32, :])
+        nc.scalar.dma_start(key_bytes[:].bitcast(I32)[0:100, :], key_bytes_dealt[:].bitcast(I32)[14:114, :])
 
         def pick_words(list_sb, name, slot):
             words = keep.tile([P, S], U32, name=name, tag=slot, align_bytes=64)
@@ -89,21 +91,20 @@ def tile_picked_kjbondduelgmid_none_p_kernel(
             nc.vector.tensor_copy(picked[:], x_bytes[:].indirect(list_sb[:]))
             return picked
 
-        b_words = pick_words(two_sb, "b_words", "b_words")
-        key_words_list = keep.tile([P, S], U32, name="key_words_list", tag="key_then_a_words", align_bytes=64)
+        key_words_list = keep.tile([P, S], U32, name="key_words_list", tag="key_list_then_w1", align_bytes=64)
         nc.vector.tensor_copy(key_words_list[:], d_tab[:].indirect(k1_sb[:]))
         key_words = keep.tile([P, S], U32, name="key_words", align_bytes=64)
         nc.vector.tensor_copy(
-            key_words[:].rearrange("p (t m) -> p t m", t=PACK),
-            key_words_list[:].rearrange("p (m t) -> p t m", t=PACK),
+            key_words[:].rearrange("p (t c i) -> p c t i", t=PACK, i=4),
+            key_words_list[:].rearrange("p (c i t) -> p c t i", t=PACK, i=4),
         )
         w2_raw = keep.tile([P, PACK, S], F32, name="w2_raw", tag="d_tab_then_w2", align_bytes=64)
         nc.sync.dma_start(w2_raw[:], w2.rearrange("(p t) m -> p t m", t=PACK))
-        w1_woven = keep.tile([P, S, PACK], BF16, name="w1_woven", align_bytes=64)
-        for half in range(2):
-            nc.scalar.copy(w1_woven[:, W * half : W * (half + 1), :], w1_halves[half][:].rearrange("p t c -> p c t"))
+        w1_raw = keep.tile([P, PACK, S], F32, name="w1_raw", tag="key_list_then_w1", align_bytes=64)
+        nc.sync.dma_start(w1_raw[:], w1.rearrange("(p t) m -> p t m", t=PACK))
+        b_words = pick_words(two_sb, "b_words", "b_words")
         b_bytes = pick_bytes(two_sb, "b_bytes")
-        a_words = pick_words(offs_sb, "a_words", "key_then_a_words")
+        a_words = pick_words(offs_sb, "a_words", "dealt_then_a_words")
         a_bytes = pick_bytes(offs_sb, "a_bytes")
 
         def score(words, scale_bytes, t, tag):
@@ -125,7 +126,7 @@ def tile_picked_kjbondduelgmid_none_p_kernel(
 
         def weave(planes, name):
             woven = keep.tile([P, S, PACK], BF16, name=name + "_woven", align_bytes=64)
-            nc.vector.tensor_copy(woven[:], planes[:].rearrange("p t c -> p c t"))
+            weave_into(nc.vector.tensor_copy, woven[:], planes[:])
             return woven
 
         def quantise(woven, name):
@@ -187,8 +188,8 @@ def tile_picked_kjbondduelgmid_none_p_kernel(
             nc.vector.tensor_scalar(z2_planes[:, t, :], placed[:], gm_sb[:, t : t + 1], None, ALU.mult)
 
         b0, diff0 = fetch_b(0, "slot0")
-        w1_q = quantise(w1_woven, "w1")
         w2_q = quantise(weave(w2_raw, "w2"), "w2")
+        w1_q = quantise(weave(w1_raw, "w1"), "w1")
         b1, diff1 = fetch_b(1, "slot1")
         a0 = fetch_a(0, "slot0")
         gate0 = gates(diff0, "slot1")
@@ -211,8 +212,8 @@ def tile_picked_kjbondduelgmid_none_p_kernel(
         place_b_scalar(gated1, 1, "slot7")
         place_b_scalar(gated2, 2, "slot7")
         z2_woven = keep.tile([P, S, PACK], BF16, name="z2_woven", align_bytes=64)
-        nc.vector.tensor_copy(z2_woven[:, :SPLIT, :], z2_planes[:, :, :SPLIT].rearrange("p t c -> p c t"))
-        nc.scalar.copy(z2_woven[:, SPLIT:, :], z2_planes[:, :, SPLIT:].rearrange("p t c -> p c t"))
+        weave_into(nc.vector.tensor_copy, z2_woven[:, :SPLIT, :], z2_planes[:, :, :SPLIT])
+        weave_into(nc.scalar.copy, z2_woven[:, SPLIT:, :], z2_planes[:, :, SPLIT:])
         z2_q = quantise(z2_woven, "z2")
 
         h_banks = []
@@ -231,15 +232,9 @@ def tile_picked_kjbondduelgmid_none_p_kernel(
                 )
             h_banks.append(bank)
 
-        h_rows = []
-        for t in range(PACK):
-            h = keep.tile([P, S + SPARE], F32, name="h%d" % t)
-            nc.gpsimd.memset(h[:, S:], 0.0)
-            if t == 0:
-                nc.scalar.copy(h[:, :S], h_banks[t][:])
-            else:
-                nc.vector.tensor_copy(h[:, :S], h_banks[t][:])
-            h_rows.append(h)
+        nc.scalar.copy(h_rows[0][:, :S], h_banks[0][:])
+        for t in range(1, PACK):
+            nc.vector.tensor_copy(h_rows[t][:, :S], h_banks[t][:])
 
         def finish_top(piece):
             h, result, start, stop, mn, mx, rows = piece
@@ -263,12 +258,7 @@ def tile_picked_kjbondduelgmid_none_p_kernel(
                     h_rows[t][:].indirect(n5_sb[:, u * PIECE // 16 : (u + 1) * PIECE // 16]),
                     ACT.Copy,
                 )
-            if t == 0:
-                cuts = [0, 128, 256, 512]
-            elif t == PACK - 1:
-                cuts = [0, 256, 384, 512]
-            else:
-                cuts = [0, 256, 512]
+            cuts = [0, 128, 256, 384, 512] if t == 0 else [0, 256, 384, 512] if t == PACK - 1 else [0, 256, 512]
             for start, stop in zip(cuts, cuts[1:]):
                 groups = stop - start
                 low = ring.tile([P, groups, 2], F32, name="low")

@@ -16,8 +16,8 @@ P = 128
 PACK = 4
 T, G, S, W = 1024, 2048, 512, 256
 SPARE = 16
-PIECE = 512
-SPLIT = 352
+EARLY = 256
+SPLIT = 320
 FLOPS = 4 * 2 * 512 * 512 * 512
 
 
@@ -50,7 +50,7 @@ def tile_picked_kjbondduelgmid_none_p_kernel(
             nc.sync.dma_start(d_bytes[:].bitcast(I32)[e:P:2, :], d_rows[e].unsqueeze(1).broadcast_to([8, 8, G // 4]))
         d_tab = keep.tile([P, G], U32, name="d_tab", tag="d_tab_then_w2", align_bytes=64)
         nc.sync.dma_start(d_tab[:].bitcast(I32), d_words[0].rearrange("p n t -> p (n t)").bitcast(I32))
-        two_sb = load_list(two, "two_sb")
+        offs_sb = load_list(offs, "offs_sb")
         x_rows = x_scales[0].bitcast(I32).rearrange("(q c) n -> c q n", c=4)
         for c, queue in enumerate((nc.sync, nc.gpsimd, nc.gpsimd, nc.gpsimd)):
             queue.dma_start(x_bytes[:].bitcast(I32)[c:P:4, :], x_rows[c].unsqueeze(1).broadcast_to([4, 8, T // 4]))
@@ -61,11 +61,11 @@ def tile_picked_kjbondduelgmid_none_p_kernel(
             nc.vector.memset(h[:, S:], 0.0)
         warm = keep.tile([P, 1], F32, name="warm")
         nc.scalar.activation(warm[:], h_rows[0][:, S : S + 1], ACT.Sigmoid)
-        offs_sb = load_list(offs, "offs_sb")
-        n3_sb = load_list(n3, "n3_sb")
-        n4_sb = load_list(n4, "n4_sb")
+        two_sb = load_list(two, "two_sb")
         n1_sb = load_list(n1, "n1_sb")
         n2_sb = load_list(n2, "n2_sb")
+        n3_sb = load_list(n3, "n3_sb")
+        n4_sb = load_list(n4, "n4_sb")
         n5_sb = load_list(n5, "n5_sb")
         gn_sb = keep.tile([P, PACK], F32, name="gn_sb")
         gm_sb = keep.tile([P, PACK], F32, name="gm_sb")
@@ -102,10 +102,10 @@ def tile_picked_kjbondduelgmid_none_p_kernel(
         nc.sync.dma_start(w2_raw[:], w2.rearrange("(p t) m -> p t m", t=PACK))
         w1_raw = keep.tile([P, PACK, S], F32, name="w1_raw", tag="key_list_then_w1", align_bytes=64)
         nc.sync.dma_start(w1_raw[:], w1.rearrange("(p t) m -> p t m", t=PACK))
-        b_words = pick_words(two_sb, "b_words", "b_words")
-        b_bytes = pick_bytes(two_sb, "b_bytes")
-        a_words = pick_words(offs_sb, "a_words", "dealt_then_a_words")
+        a_words = pick_words(offs_sb, "a_words", "a_words")
         a_bytes = pick_bytes(offs_sb, "a_bytes")
+        b_words = pick_words(two_sb, "b_words", "dealt_then_a_words")
+        b_bytes = pick_bytes(two_sb, "b_bytes")
 
         def score(words, scale_bytes, t, tag):
             cols = slice(P * t, P * (t + 1))
@@ -121,17 +121,18 @@ def tile_picked_kjbondduelgmid_none_p_kernel(
             )
             return bank
 
-        b_banks = [score(b_words, b_bytes, t, "bank%d" % t) for t in range(PACK)]
-        a_banks = [score(a_words, a_bytes, t, "bank%d" % (PACK + t)) for t in range(PACK)]
+        a_banks = [score(a_words, a_bytes, t, "bank%d" % t) for t in range(PACK)]
+        b_banks = [score(b_words, b_bytes, t, "bank%d" % (PACK + t)) for t in range(PACK)]
 
-        def weave(planes, name):
-            woven = keep.tile([P, S, PACK], BF16, name=name + "_woven", align_bytes=64)
-            weave_into(nc.vector.tensor_copy, woven[:], planes[:])
+        def weave(copy, planes, name):
+            woven = keep.tile([P, planes.shape[2], PACK], BF16, name=name + "_woven", align_bytes=64)
+            weave_into(copy, woven[:], planes)
             return woven
 
         def quantise(woven, name):
-            words = keep.tile([P, S], U32, name=name + "_words", align_bytes=64)
-            scale_bytes = keep.tile([P, S], U8, name=name + "_bytes", align_bytes=64)
+            columns = woven.shape[1]
+            words = keep.tile([P, columns], U32, name=name + "_words", align_bytes=64)
+            scale_bytes = keep.tile([P, columns], U8, name=name + "_bytes", align_bytes=64)
             nc.vector.quantize_mx(out=words[:].bitcast(FP8X4), scales=scale_bytes[:], in_=woven[:].rearrange("p c t -> p (c t)"))
             return words, scale_bytes
 
@@ -141,28 +142,28 @@ def tile_picked_kjbondduelgmid_none_p_kernel(
         def row_tile(name, slot):
             return keep.tile([P, S], F32, name=name, tag=slot)
 
-        def fetch(bank, first, second, name, slot):
-            row = row_tile(name + "_row", slot)
-            nc.scalar.activation(row[:], bank[:], ACT.Copy, scale=0.0625)
-            pair = ring.tile([P, 2 * W], F32, name=name + "_pair")
-            nc.scalar.activation(pair[:, :W], row[:].indirect(first[:]), ACT.Copy)
-            nc.scalar.activation(pair[:, W:], row[:].indirect(second[:]), ACT.Copy)
-            return pair
+        def look_up(rows, tiles, first, second, name):
+            pairs = [row_tile(name + "_pair", "%s_pair%d" % (name, t)) for t in tiles]
+            for row, pair in zip(rows, pairs):
+                nc.scalar.activation(pair[:, :W], row[:].indirect(first[:]), ACT.Copy)
+                nc.scalar.activation(pair[:, W:], row[:].indirect(second[:]), ACT.Copy)
+            return pairs
 
-        def fetch_a(t, slot):
-            return fetch(a_banks[t], n1_sb, n2_sb, "a", slot)
+        def fetch(banks, tiles, first, second, name, slots):
+            rows = [row_tile(name + "_row", slot) for slot in slots]
+            for t, row in zip(tiles, rows):
+                nc.scalar.activation(row[:], banks[t][:], ACT.Copy, scale=0.0625)
+            return look_up(rows, tiles, first, second, name)
 
-        def fetch_b(t, slot):
-            pair = fetch(b_banks[t], n3_sb, n4_sb, "b", slot)
+        def difference(pair):
             diff = ring.tile([P, W], F32, name="diff")
             nc.vector.tensor_tensor(diff[:], pair[:, :W], pair[:, W:], ALU.subtract)
-            return pair, diff
+            return diff
 
-        def bond(pair, t):
-            placed = ring.tile([P, S], F32, name="a_placed")
-            nc.vector.tensor_tensor(placed[:].indirect(n1_sb[:]), pair[:, :W], pair[:, W:], ALU.add)
-            nc.vector.tensor_tensor(placed[:].indirect(n2_sb[:]), pair[:, :W], pair[:, W:], ALU.mult)
-            nc.vector.tensor_scalar(z_planes[:, t, :], placed[:], gn_sb[:, t : t + 1], None, ALU.mult)
+        def in_turn(*chains):
+            for steps in zip(*chains):
+                for step in steps:
+                    step()
 
         def gates(diff, slot):
             gate = row_tile("gate", slot)
@@ -175,66 +176,82 @@ def tile_picked_kjbondduelgmid_none_p_kernel(
             nc.vector.tensor_tensor(gated[:], pair[:], gate[:], ALU.mult)
             return gated
 
-        def place_b_scalar(gated, t, slot):
-            placed = row_tile("b_placed", slot)
-            nc.scalar.activation(placed[:].indirect(n3_sb[:]), gated[:, :W], ACT.Copy)
-            nc.scalar.activation(placed[:].indirect(n4_sb[:]), gated[:, W:], ACT.Copy)
-            nc.scalar.activation(z2_planes[:, t, :], placed[:], ACT.Copy, scale=gm_sb[:, t : t + 1])
+        def bond_steps(pair, t, slot):
+            placed = row_tile("a_placed", slot)
+            return [
+                lambda: nc.vector.tensor_tensor(placed[:].indirect(n1_sb[:]), pair[:, :W], pair[:, W:], ALU.add),
+                lambda: nc.vector.tensor_tensor(placed[:].indirect(n2_sb[:]), pair[:, :W], pair[:, W:], ALU.mult),
+                lambda: nc.vector.tensor_scalar(z_planes[:, t, :], placed[:], gn_sb[:, t : t + 1], None, ALU.mult),
+            ]
 
-        def place_b_vector(pair, gate, t, slot):
+        def duel_scalar_steps(gated, t, slot):
             placed = row_tile("b_placed", slot)
-            nc.vector.tensor_tensor(placed[:].indirect(n3_sb[:]), pair[:, :W], gate[:, :W], ALU.mult)
-            nc.vector.tensor_tensor(placed[:].indirect(n4_sb[:]), pair[:, W:], gate[:, W:], ALU.mult)
-            nc.vector.tensor_scalar(z2_planes[:, t, :], placed[:], gm_sb[:, t : t + 1], None, ALU.mult)
+            return [
+                lambda: nc.scalar.activation(placed[:].indirect(n3_sb[:]), gated[:, :W], ACT.Copy),
+                lambda: nc.scalar.activation(placed[:].indirect(n4_sb[:]), gated[:, W:], ACT.Copy),
+                lambda: nc.scalar.activation(z2_planes[:, t, :], placed[:], ACT.Copy, scale=gm_sb[:, t : t + 1]),
+            ]
 
-        b0, diff0 = fetch_b(0, "slot0")
-        w2_q = quantise(weave(w2_raw, "w2"), "w2")
-        w1_q = quantise(weave(w1_raw, "w1"), "w1")
-        b1, diff1 = fetch_b(1, "slot1")
-        a0 = fetch_a(0, "slot0")
-        gate0 = gates(diff0, "slot1")
-        gate1 = gates(diff1, "slot0")
-        bond(a0, 0)
-        gated0 = gate_product(b0, gate0, "slot2")
-        gated1 = gate_product(b1, gate1, "slot3")
-        bond(fetch_a(1, "slot4"), 1)
-        b2, diff2 = fetch_b(2, "slot5")
-        bond(fetch_a(2, "slot6"), 2)
-        b3, diff3 = fetch_b(3, "slot7")
-        a3 = fetch_a(3, "slot8")
-        gate2 = gates(diff2, "slot8")
-        gated2 = gate_product(b2, gate2, "slot9")
-        bond(a3, 3)
-        place_b_scalar(gated0, 0, "slot7")
-        gate3 = gates(diff3, "slot2")
-        z_q = quantise(weave(z_planes, "z"), "z")
-        place_b_vector(b3, gate3, 3, "slot10")
-        place_b_scalar(gated1, 1, "slot7")
-        place_b_scalar(gated2, 2, "slot7")
+        def duel_vector_steps(pair, gate, t, slot):
+            placed = row_tile("b_placed", slot)
+            return [
+                lambda: nc.vector.tensor_tensor(placed[:].indirect(n3_sb[:]), pair[:, :W], gate[:, :W], ALU.mult),
+                lambda: nc.vector.tensor_tensor(placed[:].indirect(n4_sb[:]), pair[:, W:], gate[:, W:], ALU.mult),
+                lambda: nc.vector.tensor_scalar(z2_planes[:, t, :], placed[:], gm_sb[:, t : t + 1], None, ALU.mult),
+            ]
+
+        def run(steps):
+            for step in steps:
+                step()
+
+        a0, a1 = fetch(a_banks, (0, 1), n1_sb, n2_sb, "a", ("r0", "r1"))
+        w2_woven = weave(nc.vector.tensor_copy, w2_raw[:, :, :EARLY], "w2a")
+        late_rows = [row_tile("a_row", slot) for slot in ("r6", "r7")]
+        for t, row in zip((2, 3), late_rows):
+            nc.vector.tensor_scalar(row[:], a_banks[t][:], 0.0625, None, ALU.mult)
+        in_turn(bond_steps(a0, 0, "p0"), bond_steps(a1, 1, "p1"))
+        w2_early = quantise(w2_woven, "w2a")
+        b_pairs = fetch(b_banks, (0, 1), n3_sb, n4_sb, "b", ("r2", "r3")) + fetch(b_banks, (2, 3), n3_sb, n4_sb, "b", ("r4", "r5"))
+        diffs = [difference(pair) for pair in b_pairs]
+        w1_early = quantise(weave(nc.vector.tensor_copy, w1_raw[:, :, :EARLY], "w1a"), "w1a")
+        gate = [gates(diffs[t], "g%d" % t) for t in (0, 1)]
+        gated = [gate_product(b_pairs[t], gate[t], "gd%d" % t) for t in (0, 1)]
+        a2, a3 = look_up(late_rows, (2, 3), n1_sb, n2_sb, "a")
+        gate = gate + [gates(diffs[t], "g%d" % t) for t in (2, 3)]
+        gated.append(gate_product(b_pairs[2], gate[2], "gd2"))
+        in_turn(bond_steps(a2, 2, "p2"), bond_steps(a3, 3, "p3"), duel_vector_steps(b_pairs[3], gate[3], 3, "p4"))
+        z_q = quantise(weave(nc.vector.tensor_copy, z_planes[:], "z"), "z")
+        s0, s1, s2 = [duel_scalar_steps(gated[t], t, "q%d" % t) for t in range(3)]
+        run([s0[0], s1[0], s0[1], s1[1], s2[0], s0[2], s2[1], s1[2], s2[2]])
         z2_woven = keep.tile([P, S, PACK], BF16, name="z2_woven", align_bytes=64)
         weave_into(nc.vector.tensor_copy, z2_woven[:, :SPLIT, :], z2_planes[:, :, :SPLIT])
         weave_into(nc.scalar.copy, z2_woven[:, SPLIT:, :], z2_planes[:, :, SPLIT:])
         z2_q = quantise(z2_woven, "z2")
 
-        h_banks = []
-        for t in range(PACK):
-            cols = slice(P * t, P * (t + 1))
-            bank = psum.tile([P, S], F32, name="bank%d" % t)
-            for step, (w_q, v_q) in enumerate(((w1_q, z_q), (w2_q, z2_q))):
-                nc.tensor.matmul_mx(
-                    out=bank[:],
-                    lhsT=w_q[0][:, cols].bitcast(FP8X4),
-                    lhsT_scale=w_q[1][:, cols],
-                    rhs=v_q[0][:].bitcast(FP8X4),
-                    rhs_scale=v_q[1][:],
-                    start=(step == 0),
-                    stop=(step == 1),
-                )
-            h_banks.append(bank)
+        h_banks = [psum.tile([P, S], F32, name="bank%d" % t) for t in range(PACK)]
 
-        nc.scalar.copy(h_rows[0][:, :S], h_banks[0][:])
-        for t in range(1, PACK):
-            nc.vector.tensor_copy(h_rows[t][:, :S], h_banks[t][:])
+        def second_product(tiles, first_column, w1_q, w2_q):
+            for t in tiles:
+                for step, (w_q, v_q) in enumerate(((w1_q, z_q), (w2_q, z2_q))):
+                    cols = slice(P * t - first_column, P * (t + 1) - first_column)
+                    nc.tensor.matmul_mx(
+                        out=h_banks[t][:],
+                        lhsT=w_q[0][:, cols].bitcast(FP8X4),
+                        lhsT_scale=w_q[1][:, cols],
+                        rhs=v_q[0][:].bitcast(FP8X4),
+                        rhs_scale=v_q[1][:],
+                        start=(step == 0),
+                        stop=(step == 1),
+                    )
+
+        second_product(range(EARLY // P), 0, w1_early, w2_early)
+        w1_late_woven = keep.tile([P, S - EARLY, PACK], BF16, name="w1_late_woven", tag="z2_woven", align_bytes=64)
+        weave_into(nc.vector.tensor_copy, w1_late_woven[:], w1_raw[:, :, EARLY:])
+        w2_late_woven = keep.tile([P, S - EARLY, PACK], BF16, name="w2_late_woven", tag="z2_planes", align_bytes=64)
+        weave_into(nc.scalar.copy, w2_late_woven[:], w2_raw[:, :, EARLY:])
+        w1_late = quantise(w1_late_woven, "w1b")
+        w2_late = quantise(w2_late_woven, "w2b")
+        second_product(range(EARLY // P, PACK), EARLY, w1_late, w2_late)
 
         def finish_top(piece):
             h, result, start, stop, mn, mx, rows = piece
@@ -247,18 +264,24 @@ def tile_picked_kjbondduelgmid_none_p_kernel(
             nc.vector.scalar_tensor_tensor(result[:, start:stop], mx[:], -0.5, top[:], ALU.mult, ALU.add)
             nc.sync.dma_start(out[rows, start:stop], result[:, start:stop])
 
+        for t in (1, 2, 3):
+            nc.vector.tensor_copy(h_rows[t][:, :S], h_banks[t][:])
         previous = None
         for t in range(PACK):
+            if t not in (1, 2, 3):
+                nc.scalar.copy(h_rows[t][:, :S], h_banks[t][:])
             result = ring.tile([P, S], F32, name="result")
             members = ring.tile([P, S, PACK], F32, name="members")
             flat = members[:].rearrange("p j t -> p (j t)")
-            for u in range(G // PIECE):
-                nc.scalar.activation(
-                    flat[:, PIECE * u : PIECE * (u + 1)],
-                    h_rows[t][:].indirect(n5_sb[:, u * PIECE // 16 : (u + 1) * PIECE // 16]),
-                    ACT.Copy,
-                )
-            cuts = [0, 128, 256, 384, 512] if t == 0 else [0, 256, 384, 512] if t == PACK - 1 else [0, 256, 512]
+            gcuts = [[0,128,256,384,512],[0,128,256,384,512],[0,128,256,384,512],[0,128,256,384,512]][t]
+            for start, stop in zip(gcuts, gcuts[1:]):
+                picked = flat[:, PACK * start : PACK * stop]
+                window = h_rows[t][:].indirect(n5_sb[:, start // 4 : stop // 4])
+                if (t, start) in ((0, 128),):
+                    nc.vector.tensor_copy(picked, window)
+                else:
+                    nc.scalar.activation(picked, window, ACT.Copy)
+            cuts = [[0,256,512],[0,256,512],[0,256,512],[0,256,512]][t]
             for start, stop in zip(cuts, cuts[1:]):
                 groups = stop - start
                 low = ring.tile([P, groups, 2], F32, name="low")

@@ -15,7 +15,12 @@ ACT = mybir.ActivationFunctionType
 P = 128
 PACK = 4
 T, G, S, W = 1024, 2048, 512, 256
+MEMBERS = 4
+LIST_ROWS = 16
+SCORE_SCALE = 0.0625
 SPARE = 16
+GATHER = 512
+HALF = S // 2
 EARLY = 256
 SPLIT = 320
 FLOPS = 4 * 2 * 512 * 512 * 512
@@ -28,7 +33,7 @@ def tile_picked_kjbondduelgmid_none_p_kernel(
     with ExitStack() as ctx:
         lists = ctx.enter_context(tc.tile_pool(name="lists", bufs=1))
         keep = ctx.enter_context(tc.tile_pool(name="keep", bufs=1))
-        ring = ctx.enter_context(tc.tile_pool(name="ring", bufs=4))
+        ring = ctx.enter_context(tc.tile_pool(name="ring", bufs=PACK))
         psum = ctx.enter_context(tc.psum_pool(name="psum", bufs=1))
 
         def load_list(src, name):
@@ -45,20 +50,17 @@ def tile_picked_kjbondduelgmid_none_p_kernel(
         key_bytes = keep.tile([P, S], U8, name="key_bytes", align_bytes=64)
 
         k1_sb = load_list(k1, "k1_sb")
-        d_rows = d_scales[0].bitcast(I32).rearrange("(r e) n -> e r n", e=2)
-        for e in range(2):
-            nc.sync.dma_start(d_bytes[:].bitcast(I32)[e:P:2, :], d_rows[e].unsqueeze(1).broadcast_to([8, 8, G // 4]))
+        nc.sync.dma_start(d_bytes[:].bitcast(I32), d_scales[0].bitcast(I32).unsqueeze(1).broadcast_to([16, 8, G // 4]))
         d_tab = keep.tile([P, G], U32, name="d_tab", tag="d_tab_then_w2", align_bytes=64)
         nc.sync.dma_start(d_tab[:].bitcast(I32), d_words[0].rearrange("p n t -> p (n t)").bitcast(I32))
         offs_sb = load_list(offs, "offs_sb")
         x_rows = x_scales[0].bitcast(I32).rearrange("(q c) n -> c q n", c=4)
-        for c, queue in enumerate((nc.sync, nc.gpsimd, nc.gpsimd, nc.gpsimd)):
+        for c, queue in enumerate((nc.sync, nc.sync, nc.gpsimd, nc.gpsimd)):
             queue.dma_start(x_bytes[:].bitcast(I32)[c:P:4, :], x_rows[c].unsqueeze(1).broadcast_to([4, 8, T // 4]))
         x_tab = keep.tile([P, T], U32, name="x_tab", align_bytes=64)
         nc.sync.dma_start(x_tab[:].bitcast(I32), x_words[0].rearrange("p n t -> p (n t)").bitcast(I32))
-        nc.vector.memset(key_bytes[:].bitcast(I32), 0)
-        for h in h_rows:
-            nc.vector.memset(h[:, S:], 0.0)
+        for h_row in h_rows:
+            nc.vector.memset(h_row[:, S:], 0.0)
         warm = keep.tile([P, 1], F32, name="warm")
         nc.scalar.activation(warm[:], h_rows[0][:, S : S + 1], ACT.Sigmoid)
         two_sb = load_list(two, "two_sb")
@@ -74,15 +76,15 @@ def tile_picked_kjbondduelgmid_none_p_kernel(
 
         key_bytes_list = keep.tile([P, S], U8, name="key_bytes_list", align_bytes=64)
         nc.vector.tensor_copy(key_bytes_list[:], d_bytes[:].indirect(k1_sb[:]))
-        key_bytes_dealt = keep.tile([P, S], U8, name="key_bytes_dealt", tag="dealt_then_a_words", align_bytes=64)
         nc.vector.tensor_copy(
-            key_bytes_dealt[:].rearrange("p (t c i) -> p c t i", t=PACK, i=16),
+            key_bytes[:].rearrange("p (t c i) -> p c t i", t=PACK, i=16),
             key_bytes_list[:].rearrange("p (c i t) -> p c t i", t=PACK, i=16),
         )
-        nc.scalar.dma_start(key_bytes[:].bitcast(I32)[0:100, :], key_bytes_dealt[:].bitcast(I32)[14:114, :])
+        for c in range(1, 4):
+            nc.scalar.dma_start(key_bytes[:].bitcast(I32)[c:P:32, :], key_bytes[:].bitcast(I32)[8 * c : P : 32, :])
 
-        def pick_words(list_sb, name, slot):
-            words = keep.tile([P, S], U32, name=name, tag=slot, align_bytes=64)
+        def pick_words(list_sb, name):
+            words = keep.tile([P, S], U32, name=name, align_bytes=64)
             nc.vector.tensor_copy(words[:], x_tab[:].indirect(list_sb[:]))
             return words
 
@@ -102,14 +104,14 @@ def tile_picked_kjbondduelgmid_none_p_kernel(
         nc.sync.dma_start(w2_raw[:], w2.rearrange("(p t) m -> p t m", t=PACK))
         w1_raw = keep.tile([P, PACK, S], F32, name="w1_raw", tag="key_list_then_w1", align_bytes=64)
         nc.sync.dma_start(w1_raw[:], w1.rearrange("(p t) m -> p t m", t=PACK))
-        a_words = pick_words(offs_sb, "a_words", "a_words")
+        a_words = pick_words(offs_sb, "a_words")
         a_bytes = pick_bytes(offs_sb, "a_bytes")
-        b_words = pick_words(two_sb, "b_words", "dealt_then_a_words")
+        b_words = pick_words(two_sb, "b_words")
         b_bytes = pick_bytes(two_sb, "b_bytes")
 
-        def score(words, scale_bytes, t, tag):
+        def score(words, scale_bytes, t, bank_number):
             cols = slice(P * t, P * (t + 1))
-            bank = psum.tile([P, S], F32, name=tag)
+            bank = psum.tile([P, S], F32, name="bank%d" % bank_number)
             nc.tensor.matmul_mx(
                 out=bank[:],
                 lhsT=key_words[:, cols].bitcast(FP8X4),
@@ -121,38 +123,40 @@ def tile_picked_kjbondduelgmid_none_p_kernel(
             )
             return bank
 
-        a_banks = [score(a_words, a_bytes, t, "bank%d" % t) for t in range(PACK)]
-        b_banks = [score(b_words, b_bytes, t, "bank%d" % (PACK + t)) for t in range(PACK)]
+        a_banks = [score(a_words, a_bytes, t, t) for t in range(PACK)]
+        b_banks = [score(b_words, b_bytes, t, PACK + t) for t in range(PACK)]
 
-        def weave(copy, planes, name):
+        def weave(planes, name):
             woven = keep.tile([P, planes.shape[2], PACK], BF16, name=name + "_woven", align_bytes=64)
-            weave_into(copy, woven[:], planes)
+            weave_into(nc.vector.tensor_copy, woven[:], planes)
             return woven
 
         def quantise(woven, name):
             columns = woven.shape[1]
             words = keep.tile([P, columns], U32, name=name + "_words", align_bytes=64)
             scale_bytes = keep.tile([P, columns], U8, name=name + "_bytes", align_bytes=64)
-            nc.vector.quantize_mx(out=words[:].bitcast(FP8X4), scales=scale_bytes[:], in_=woven[:].rearrange("p c t -> p (c t)"))
+            nc.vector.quantize_mx(
+                out=words[:].bitcast(FP8X4), scales=scale_bytes[:], in_=woven[:].rearrange("p c t -> p (c t)")
+            )
             return words, scale_bytes
 
         z_planes = keep.tile([P, PACK, S], BF16, name="z_planes", align_bytes=64)
         z2_planes = keep.tile([P, PACK, S], BF16, name="z2_planes", align_bytes=64)
 
-        def row_tile(name, slot):
-            return keep.tile([P, S], F32, name=name, tag=slot)
+        def row_tile(name, t):
+            return keep.tile([P, S], F32, name="%s%d" % (name, t))
 
         def look_up(rows, tiles, first, second, name):
-            pairs = [row_tile(name + "_pair", "%s_pair%d" % (name, t)) for t in tiles]
+            pairs = [row_tile(name + "_pair", t) for t in tiles]
             for row, pair in zip(rows, pairs):
                 nc.scalar.activation(pair[:, :W], row[:].indirect(first[:]), ACT.Copy)
                 nc.scalar.activation(pair[:, W:], row[:].indirect(second[:]), ACT.Copy)
             return pairs
 
-        def fetch(banks, tiles, first, second, name, slots):
-            rows = [row_tile(name + "_row", slot) for slot in slots]
+        def fetch(banks, tiles, first, second, name):
+            rows = [row_tile(name + "_row", t) for t in tiles]
             for t, row in zip(tiles, rows):
-                nc.scalar.activation(row[:], banks[t][:], ACT.Copy, scale=0.0625)
+                nc.scalar.activation(row[:], banks[t][:], ACT.Copy, scale=SCORE_SCALE)
             return look_up(rows, tiles, first, second, name)
 
         def difference(pair):
@@ -160,69 +164,68 @@ def tile_picked_kjbondduelgmid_none_p_kernel(
             nc.vector.tensor_tensor(diff[:], pair[:, :W], pair[:, W:], ALU.subtract)
             return diff
 
-        def in_turn(*chains):
-            for steps in zip(*chains):
-                for step in steps:
-                    step()
-
-        def gates(diff, slot):
-            gate = row_tile("gate", slot)
+        def sigmoids(diff, t):
+            gate = row_tile("gate", t)
             nc.scalar.activation(gate[:, :W], diff[:], ACT.Sigmoid)
             nc.scalar.activation(gate[:, W:], diff[:], ACT.Sigmoid, scale=-1.0)
             return gate
 
-        def gate_product(pair, gate, slot):
-            gated = row_tile("gated", slot)
+        def gate_product(pair, gate, t):
+            gated = row_tile("gated", t)
             nc.vector.tensor_tensor(gated[:], pair[:], gate[:], ALU.mult)
             return gated
 
-        def bond_steps(pair, t, slot):
-            placed = row_tile("a_placed", slot)
+        def place_a(pair, t):
+            placed = row_tile("a_placed", t)
             return [
                 lambda: nc.vector.tensor_tensor(placed[:].indirect(n1_sb[:]), pair[:, :W], pair[:, W:], ALU.add),
                 lambda: nc.vector.tensor_tensor(placed[:].indirect(n2_sb[:]), pair[:, :W], pair[:, W:], ALU.mult),
                 lambda: nc.vector.tensor_scalar(z_planes[:, t, :], placed[:], gn_sb[:, t : t + 1], None, ALU.mult),
             ]
 
-        def duel_scalar_steps(gated, t, slot):
-            placed = row_tile("b_placed", slot)
+        def place_b_on_scalar(gated, t):
+            placed = row_tile("b_placed", t)
             return [
                 lambda: nc.scalar.activation(placed[:].indirect(n3_sb[:]), gated[:, :W], ACT.Copy),
                 lambda: nc.scalar.activation(placed[:].indirect(n4_sb[:]), gated[:, W:], ACT.Copy),
                 lambda: nc.scalar.activation(z2_planes[:, t, :], placed[:], ACT.Copy, scale=gm_sb[:, t : t + 1]),
             ]
 
-        def duel_vector_steps(pair, gate, t, slot):
-            placed = row_tile("b_placed", slot)
+        def place_b_on_vector(pair, gate, t):
+            placed = row_tile("b_placed", t)
             return [
                 lambda: nc.vector.tensor_tensor(placed[:].indirect(n3_sb[:]), pair[:, :W], gate[:, :W], ALU.mult),
                 lambda: nc.vector.tensor_tensor(placed[:].indirect(n4_sb[:]), pair[:, W:], gate[:, W:], ALU.mult),
                 lambda: nc.vector.tensor_scalar(z2_planes[:, t, :], placed[:], gm_sb[:, t : t + 1], None, ALU.mult),
             ]
 
-        def run(steps):
-            for step in steps:
-                step()
+        def in_turn(*chains):
+            for steps in zip(*chains):
+                for step in steps:
+                    step()
 
-        a0, a1 = fetch(a_banks, (0, 1), n1_sb, n2_sb, "a", ("r0", "r1"))
-        w2_woven = weave(nc.vector.tensor_copy, w2_raw[:, :, :EARLY], "w2a")
-        late_rows = [row_tile("a_row", slot) for slot in ("r6", "r7")]
-        for t, row in zip((2, 3), late_rows):
-            nc.vector.tensor_scalar(row[:], a_banks[t][:], 0.0625, None, ALU.mult)
-        in_turn(bond_steps(a0, 0, "p0"), bond_steps(a1, 1, "p1"))
-        w2_early = quantise(w2_woven, "w2a")
-        b_pairs = fetch(b_banks, (0, 1), n3_sb, n4_sb, "b", ("r2", "r3")) + fetch(b_banks, (2, 3), n3_sb, n4_sb, "b", ("r4", "r5"))
+        first_two, last_two = (0, 1), (2, 3)
+        a0, a1 = fetch(a_banks, first_two, n1_sb, n2_sb, "a")
+        w2_early_woven = weave(w2_raw[:, :, :EARLY], "w2_early")
+        a_last_rows = [row_tile("a_row", t) for t in last_two]
+        for t, row in zip(last_two, a_last_rows):
+            nc.vector.tensor_scalar(row[:], a_banks[t][:], SCORE_SCALE, None, ALU.mult)
+        in_turn(place_a(a0, 0), place_a(a1, 1))
+        w2_early = quantise(w2_early_woven, "w2_early")
+        b_pairs = fetch(b_banks, first_two, n3_sb, n4_sb, "b") + fetch(b_banks, last_two, n3_sb, n4_sb, "b")
         diffs = [difference(pair) for pair in b_pairs]
-        w1_early = quantise(weave(nc.vector.tensor_copy, w1_raw[:, :, :EARLY], "w1a"), "w1a")
-        gate = [gates(diffs[t], "g%d" % t) for t in (0, 1)]
-        gated = [gate_product(b_pairs[t], gate[t], "gd%d" % t) for t in (0, 1)]
-        a2, a3 = look_up(late_rows, (2, 3), n1_sb, n2_sb, "a")
-        gate = gate + [gates(diffs[t], "g%d" % t) for t in (2, 3)]
-        gated.append(gate_product(b_pairs[2], gate[2], "gd2"))
-        in_turn(bond_steps(a2, 2, "p2"), bond_steps(a3, 3, "p3"), duel_vector_steps(b_pairs[3], gate[3], 3, "p4"))
-        z_q = quantise(weave(nc.vector.tensor_copy, z_planes[:], "z"), "z")
-        s0, s1, s2 = [duel_scalar_steps(gated[t], t, "q%d" % t) for t in range(3)]
-        run([s0[0], s1[0], s0[1], s1[1], s2[0], s0[2], s2[1], s1[2], s2[2]])
+        w1_early = quantise(weave(w1_raw[:, :, :EARLY], "w1_early"), "w1_early")
+        gates = [sigmoids(diffs[t], t) for t in first_two]
+        gated = [gate_product(b_pairs[t], gates[t], t) for t in first_two]
+        a2, a3 = look_up(a_last_rows, last_two, n1_sb, n2_sb, "a")
+        gates = gates + [sigmoids(diffs[t], t) for t in last_two]
+        gated.append(gate_product(b_pairs[2], gates[2], 2))
+        in_turn(place_a(a2, 2), place_a(a3, 3), place_b_on_vector(b_pairs[3], gates[3], 3))
+        z_q = quantise(weave(z_planes[:], "z"), "z")
+        b0_steps, b1_steps, b2_steps = [place_b_on_scalar(gated[t], t) for t in range(3)]
+        in_turn(b0_steps[:2], b1_steps[:2])
+        in_turn(b2_steps[:2], [b0_steps[2], b1_steps[2]])
+        b2_steps[2]()
         z2_woven = keep.tile([P, S, PACK], BF16, name="z2_woven", align_bytes=64)
         weave_into(nc.vector.tensor_copy, z2_woven[:, :SPLIT, :], z2_planes[:, :, :SPLIT])
         weave_into(nc.scalar.copy, z2_woven[:, SPLIT:, :], z2_planes[:, :, SPLIT:])
@@ -249,52 +252,48 @@ def tile_picked_kjbondduelgmid_none_p_kernel(
         weave_into(nc.vector.tensor_copy, w1_late_woven[:], w1_raw[:, :, EARLY:])
         w2_late_woven = keep.tile([P, S - EARLY, PACK], BF16, name="w2_late_woven", tag="z2_planes", align_bytes=64)
         weave_into(nc.scalar.copy, w2_late_woven[:], w2_raw[:, :, EARLY:])
-        w1_late = quantise(w1_late_woven, "w1b")
-        w2_late = quantise(w2_late_woven, "w2b")
+        w1_late = quantise(w1_late_woven, "w1_late")
+        w2_late = quantise(w2_late_woven, "w2_late")
         second_product(range(EARLY // P, PACK), EARLY, w1_late, w2_late)
 
-        def finish_top(piece):
-            h, result, start, stop, mn, mx, rows = piece
-            top = ring.tile([P, stop - start], F32, name="top")
-            nc.vector.tensor_tensor(top[:], h[:, start:stop], mn[:], ALU.max)
+        def larger_of_h_and_smallest(piece):
+            t, cols, result, smallest, largest = piece
+            top = ring.tile([P, HALF], F32, name="top")
+            nc.vector.tensor_tensor(top[:], h_rows[t][:, cols], smallest[:], ALU.max)
             return top
 
-        def finish_out(piece, top):
-            h, result, start, stop, mn, mx, rows = piece
-            nc.vector.scalar_tensor_tensor(result[:, start:stop], mx[:], -0.5, top[:], ALU.mult, ALU.add)
-            nc.sync.dma_start(out[rows, start:stop], result[:, start:stop])
+        def store(piece, top):
+            t, cols, result, smallest, largest = piece
+            nc.vector.scalar_tensor_tensor(result[:, cols], largest[:], -0.5, top[:], ALU.mult, ALU.add)
+            nc.sync.dma_start(out[P * t : P * (t + 1), cols], result[:, cols])
 
-        for t in (1, 2, 3):
+        for t in range(1, PACK):
             nc.vector.tensor_copy(h_rows[t][:, :S], h_banks[t][:])
+        nc.scalar.copy(h_rows[0][:, :S], h_banks[0][:])
         previous = None
         for t in range(PACK):
-            if t not in (1, 2, 3):
-                nc.scalar.copy(h_rows[t][:, :S], h_banks[t][:])
             result = ring.tile([P, S], F32, name="result")
-            members = ring.tile([P, S, PACK], F32, name="members")
-            flat = members[:].rearrange("p j t -> p (j t)")
-            gcuts = [[0,128,256,384,512],[0,128,256,384,512],[0,128,256,384,512],[0,128,256,384,512]][t]
-            for start, stop in zip(gcuts, gcuts[1:]):
-                picked = flat[:, PACK * start : PACK * stop]
-                window = h_rows[t][:].indirect(n5_sb[:, start // 4 : stop // 4])
-                if (t, start) in ((0, 128),):
-                    nc.vector.tensor_copy(picked, window)
+            members = ring.tile([P, S, MEMBERS], F32, name="members")
+            entries = members[:].rearrange("p j u -> p (j u)")
+            for first in range(0, S * MEMBERS, GATHER):
+                window = h_rows[t][:].indirect(n5_sb[:, first // LIST_ROWS : (first + GATHER) // LIST_ROWS])
+                if t == 0 and first == GATHER:
+                    nc.vector.tensor_copy(entries[:, first : first + GATHER], window)
                 else:
-                    nc.scalar.activation(picked, window, ACT.Copy)
-            cuts = [[0,256,512],[0,256,512],[0,256,512],[0,256,512]][t]
-            for start, stop in zip(cuts, cuts[1:]):
-                groups = stop - start
-                low = ring.tile([P, groups, 2], F32, name="low")
-                high = ring.tile([P, groups, 2], F32, name="high")
-                mn = ring.tile([P, groups], F32, name="mn")
-                mx = ring.tile([P, groups], F32, name="mx")
-                nc.vector.tensor_tensor(low[:], members[:, start:stop, 0:2], members[:, start:stop, 2:4], ALU.min)
-                nc.vector.tensor_tensor(high[:], members[:, start:stop, 0:2], members[:, start:stop, 2:4], ALU.max)
+                    nc.scalar.activation(entries[:, first : first + GATHER], window, ACT.Copy)
+            for first in range(0, S, HALF):
+                cols = slice(first, first + HALF)
+                low = ring.tile([P, HALF, 2], F32, name="low")
+                high = ring.tile([P, HALF, 2], F32, name="high")
+                smallest = ring.tile([P, HALF], F32, name="smallest")
+                largest = ring.tile([P, HALF], F32, name="largest")
+                nc.vector.tensor_tensor(low[:], members[:, cols, 0:2], members[:, cols, 2:4], ALU.min)
+                nc.vector.tensor_tensor(high[:], members[:, cols, 0:2], members[:, cols, 2:4], ALU.max)
                 if previous is not None:
-                    top = finish_top(previous)
-                nc.vector.tensor_tensor(mn[:], low[:, :, 0], low[:, :, 1], ALU.min)
+                    top = larger_of_h_and_smallest(previous)
+                nc.vector.tensor_tensor(smallest[:], low[:, :, 0], low[:, :, 1], ALU.min)
                 if previous is not None:
-                    finish_out(previous, top)
-                nc.vector.tensor_tensor(mx[:], high[:, :, 0], high[:, :, 1], ALU.max)
-                previous = (h_rows[t], result, start, stop, mn, mx, slice(P * t, P * (t + 1)))
-        finish_out(previous, finish_top(previous))
+                    store(previous, top)
+                nc.vector.tensor_tensor(largest[:], high[:, :, 0], high[:, :, 1], ALU.max)
+                previous = (t, cols, result, smallest, largest)
+        store(previous, larger_of_h_and_smallest(previous))

from contextlib import ExitStack

import concourse.mybir as mybir

F32 = mybir.dt.float32
BF16 = mybir.dt.bfloat16
I32 = mybir.dt.int32
U32 = mybir.dt.uint32
U16 = mybir.dt.uint16
U8 = mybir.dt.uint8
FP8X4 = mybir.dt.float8_e4m3fn_x4
ALU = mybir.AluOpType
ACT = mybir.ActivationFunctionType

P = 128
PACK = 4
T, G, S, W = 1024, 2048, 512, 256
MEMBERS = 4
LIST_ROWS = 16
SCORE_SCALE = 0.0625
SPARE = 16
GATHER = 512
HALF = S // 2
EARLY = 256
SPLIT = 320
FLOPS = 4 * 2 * 512 * 512 * 512


def tile_picked_kjbondduelgmid_none_p_kernel(
    tc, x_words, x_scales, d_words, d_scales, gn, gm, w1, w2, offs, k1, two, n1, n2, n3, n4, n5, out
):
    nc = tc.nc
    with ExitStack() as ctx:
        lists = ctx.enter_context(tc.tile_pool(name="lists", bufs=1))
        keep = ctx.enter_context(tc.tile_pool(name="keep", bufs=1))
        ring = ctx.enter_context(tc.tile_pool(name="ring", bufs=PACK))
        psum = ctx.enter_context(tc.psum_pool(name="psum", bufs=1))

        def load_list(src, name):
            tile = lists.tile(list(src.shape), U16, name=name)
            nc.sync.dma_start(tile[:], src)
            return tile

        def weave_into(copy, woven, planes):
            copy(woven.rearrange("p (c i) t -> p c t i", i=4), planes.rearrange("p t (c i) -> p c t i", i=4))

        h_rows = [keep.tile([P, S + SPARE], F32, name="h%d" % t) for t in range(PACK)]
        d_bytes = keep.tile([P, G], U8, name="d_bytes", align_bytes=64)
        x_bytes = keep.tile([P, T], U8, name="x_bytes", align_bytes=64)
        key_bytes = keep.tile([P, S], U8, name="key_bytes", align_bytes=64)

        k1_sb = load_list(k1, "k1_sb")
        nc.sync.dma_start(d_bytes[:].bitcast(I32), d_scales[0].bitcast(I32).unsqueeze(1).broadcast_to([16, 8, G // 4]))
        d_tab = keep.tile([P, G], U32, name="d_tab", tag="d_tab_then_w2", align_bytes=64)
        nc.sync.dma_start(d_tab[:].bitcast(I32), d_words[0].rearrange("p n t -> p (n t)").bitcast(I32))
        offs_sb = load_list(offs, "offs_sb")
        x_rows = x_scales[0].bitcast(I32).rearrange("(q c) n -> c q n", c=4)
        for c, queue in enumerate((nc.sync, nc.sync, nc.gpsimd, nc.gpsimd)):
            queue.dma_start(x_bytes[:].bitcast(I32)[c:P:4, :], x_rows[c].unsqueeze(1).broadcast_to([4, 8, T // 4]))
        x_tab = keep.tile([P, T], U32, name="x_tab", align_bytes=64)
        nc.sync.dma_start(x_tab[:].bitcast(I32), x_words[0].rearrange("p n t -> p (n t)").bitcast(I32))
        for h_row in h_rows:
            nc.vector.memset(h_row[:, S:], 0.0)
        warm = keep.tile([P, 1], F32, name="warm")
        nc.scalar.activation(warm[:], h_rows[0][:, S : S + 1], ACT.Sigmoid)
        two_sb = load_list(two, "two_sb")
        n1_sb = load_list(n1, "n1_sb")
        n2_sb = load_list(n2, "n2_sb")
        n3_sb = load_list(n3, "n3_sb")
        n4_sb = load_list(n4, "n4_sb")
        n5_sb = load_list(n5, "n5_sb")
        gn_sb = keep.tile([P, PACK], F32, name="gn_sb")
        gm_sb = keep.tile([P, PACK], F32, name="gm_sb")
        nc.gpsimd.dma_start(gn_sb[:], gn.rearrange("(p t) o -> p (t o)", t=PACK))
        nc.gpsimd.dma_start(gm_sb[:], gm.rearrange("(p t) o -> p (t o)", t=PACK))

        key_bytes_list = keep.tile([P, S], U8, name="key_bytes_list", align_bytes=64)
        nc.vector.tensor_copy(key_bytes_list[:], d_bytes[:].indirect(k1_sb[:]))
        nc.vector.tensor_copy(
            key_bytes[:].rearrange("p (t c i) -> p c t i", t=PACK, i=16),
            key_bytes_list[:].rearrange("p (c i t) -> p c t i", t=PACK, i=16),
        )
        for c in range(1, 4):
            nc.scalar.dma_start(key_bytes[:].bitcast(I32)[c:P:32, :], key_bytes[:].bitcast(I32)[8 * c : P : 32, :])

        def pick_words(list_sb, name):
            words = keep.tile([P, S], U32, name=name, align_bytes=64)
            nc.vector.tensor_copy(words[:], x_tab[:].indirect(list_sb[:]))
            return words

        def pick_bytes(list_sb, name):
            picked = keep.tile([P, S], U8, name=name, align_bytes=64)
            nc.vector.tensor_copy(picked[:], x_bytes[:].indirect(list_sb[:]))
            return picked

        key_words_list = keep.tile([P, S], U32, name="key_words_list", tag="key_list_then_w1", align_bytes=64)
        nc.vector.tensor_copy(key_words_list[:], d_tab[:].indirect(k1_sb[:]))
        key_words = keep.tile([P, S], U32, name="key_words", align_bytes=64)
        nc.vector.tensor_copy(
            key_words[:].rearrange("p (t c i) -> p c t i", t=PACK, i=4),
            key_words_list[:].rearrange("p (c i t) -> p c t i", t=PACK, i=4),
        )
        w2_raw = keep.tile([P, PACK, S], F32, name="w2_raw", tag="d_tab_then_w2", align_bytes=64)
        nc.sync.dma_start(w2_raw[:], w2.rearrange("(p t) m -> p t m", t=PACK))
        w1_raw = keep.tile([P, PACK, S], F32, name="w1_raw", tag="key_list_then_w1", align_bytes=64)
        nc.sync.dma_start(w1_raw[:], w1.rearrange("(p t) m -> p t m", t=PACK))
        a_words = pick_words(offs_sb, "a_words")
        a_bytes = pick_bytes(offs_sb, "a_bytes")
        b_words = pick_words(two_sb, "b_words")
        b_bytes = pick_bytes(two_sb, "b_bytes")

        def score(words, scale_bytes, t, bank_number):
            cols = slice(P * t, P * (t + 1))
            bank = psum.tile([P, S], F32, name="bank%d" % bank_number)
            nc.tensor.matmul_mx(
                out=bank[:],
                lhsT=key_words[:, cols].bitcast(FP8X4),
                lhsT_scale=key_bytes[:, cols],
                rhs=words[:].bitcast(FP8X4),
                rhs_scale=scale_bytes[:],
                start=True,
                stop=True,
            )
            return bank

        a_banks = [score(a_words, a_bytes, t, t) for t in range(PACK)]
        b_banks = [score(b_words, b_bytes, t, PACK + t) for t in range(PACK)]

        def weave(planes, name):
            woven = keep.tile([P, planes.shape[2], PACK], BF16, name=name + "_woven", align_bytes=64)
            weave_into(nc.vector.tensor_copy, woven[:], planes)
            return woven

        def quantise(woven, name):
            columns = woven.shape[1]
            words = keep.tile([P, columns], U32, name=name + "_words", align_bytes=64)
            scale_bytes = keep.tile([P, columns], U8, name=name + "_bytes", align_bytes=64)
            nc.vector.quantize_mx(
                out=words[:].bitcast(FP8X4), scales=scale_bytes[:], in_=woven[:].rearrange("p c t -> p (c t)")
            )
            return words, scale_bytes

        z_planes = keep.tile([P, PACK, S], BF16, name="z_planes", align_bytes=64)
        z2_planes = keep.tile([P, PACK, S], BF16, name="z2_planes", align_bytes=64)

        def row_tile(name, t):
            return keep.tile([P, S], F32, name="%s%d" % (name, t))

        def look_up(rows, tiles, first, second, name):
            pairs = [row_tile(name + "_pair", t) for t in tiles]
            for row, pair in zip(rows, pairs):
                nc.scalar.activation(pair[:, :W], row[:].indirect(first[:]), ACT.Copy)
                nc.scalar.activation(pair[:, W:], row[:].indirect(second[:]), ACT.Copy)
            return pairs

        def fetch(banks, tiles, first, second, name):
            rows = [row_tile(name + "_row", t) for t in tiles]
            for t, row in zip(tiles, rows):
                nc.scalar.activation(row[:], banks[t][:], ACT.Copy, scale=SCORE_SCALE)
            return look_up(rows, tiles, first, second, name)

        def difference(pair):
            diff = ring.tile([P, W], F32, name="diff")
            nc.vector.tensor_tensor(diff[:], pair[:, :W], pair[:, W:], ALU.subtract)
            return diff

        def sigmoids(diff, t):
            gate = row_tile("gate", t)
            nc.scalar.activation(gate[:, :W], diff[:], ACT.Sigmoid)
            nc.scalar.activation(gate[:, W:], diff[:], ACT.Sigmoid, scale=-1.0)
            return gate

        def gate_product(pair, gate, t):
            gated = row_tile("gated", t)
            nc.vector.tensor_tensor(gated[:], pair[:], gate[:], ALU.mult)
            return gated

        def place_a(pair, t):
            placed = row_tile("a_placed", t)
            return [
                lambda: nc.vector.tensor_tensor(placed[:].indirect(n1_sb[:]), pair[:, :W], pair[:, W:], ALU.add),
                lambda: nc.vector.tensor_tensor(placed[:].indirect(n2_sb[:]), pair[:, :W], pair[:, W:], ALU.mult),
                lambda: nc.vector.tensor_scalar(z_planes[:, t, :], placed[:], gn_sb[:, t : t + 1], None, ALU.mult),
            ]

        def place_b_on_scalar(gated, t):
            placed = row_tile("b_placed", t)
            return [
                lambda: nc.scalar.activation(placed[:].indirect(n3_sb[:]), gated[:, :W], ACT.Copy),
                lambda: nc.scalar.activation(placed[:].indirect(n4_sb[:]), gated[:, W:], ACT.Copy),
                lambda: nc.scalar.activation(z2_planes[:, t, :], placed[:], ACT.Copy, scale=gm_sb[:, t : t + 1]),
            ]

        def place_b_on_vector(pair, gate, t):
            placed = row_tile("b_placed", t)
            return [
                lambda: nc.vector.tensor_tensor(placed[:].indirect(n3_sb[:]), pair[:, :W], gate[:, :W], ALU.mult),
                lambda: nc.vector.tensor_tensor(placed[:].indirect(n4_sb[:]), pair[:, W:], gate[:, W:], ALU.mult),
                lambda: nc.vector.tensor_scalar(z2_planes[:, t, :], placed[:], gm_sb[:, t : t + 1], None, ALU.mult),
            ]

        def in_turn(*chains):
            for steps in zip(*chains):
                for step in steps:
                    step()

        first_two, last_two = (0, 1), (2, 3)
        a0, a1 = fetch(a_banks, first_two, n1_sb, n2_sb, "a")
        w2_early_woven = weave(w2_raw[:, :, :EARLY], "w2_early")
        a_last_rows = [row_tile("a_row", t) for t in last_two]
        for t, row in zip(last_two, a_last_rows):
            nc.vector.tensor_scalar(row[:], a_banks[t][:], SCORE_SCALE, None, ALU.mult)
        in_turn(place_a(a0, 0), place_a(a1, 1))
        w2_early = quantise(w2_early_woven, "w2_early")
        b_pairs = fetch(b_banks, first_two, n3_sb, n4_sb, "b") + fetch(b_banks, last_two, n3_sb, n4_sb, "b")
        diffs = [difference(pair) for pair in b_pairs]
        w1_early = quantise(weave(w1_raw[:, :, :EARLY], "w1_early"), "w1_early")
        gates = [sigmoids(diffs[t], t) for t in first_two]
        gated = [gate_product(b_pairs[t], gates[t], t) for t in first_two]
        a2, a3 = look_up(a_last_rows, last_two, n1_sb, n2_sb, "a")
        gates = gates + [sigmoids(diffs[t], t) for t in last_two]
        gated.append(gate_product(b_pairs[2], gates[2], 2))
        in_turn(place_a(a2, 2), place_a(a3, 3), place_b_on_vector(b_pairs[3], gates[3], 3))
        z_q = quantise(weave(z_planes[:], "z"), "z")
        b0_steps, b1_steps, b2_steps = [place_b_on_scalar(gated[t], t) for t in range(3)]
        in_turn(b0_steps[:2], b1_steps[:2])
        in_turn(b2_steps[:2], [b0_steps[2], b1_steps[2]])
        b2_steps[2]()
        z2_woven = keep.tile([P, S, PACK], BF16, name="z2_woven", align_bytes=64)
        weave_into(nc.vector.tensor_copy, z2_woven[:, :SPLIT, :], z2_planes[:, :, :SPLIT])
        weave_into(nc.scalar.copy, z2_woven[:, SPLIT:, :], z2_planes[:, :, SPLIT:])
        z2_q = quantise(z2_woven, "z2")

        h_banks = [psum.tile([P, S], F32, name="bank%d" % t) for t in range(PACK)]

        def second_product(tiles, first_column, w1_q, w2_q):
            for t in tiles:
                for step, (w_q, v_q) in enumerate(((w1_q, z_q), (w2_q, z2_q))):
                    cols = slice(P * t - first_column, P * (t + 1) - first_column)
                    nc.tensor.matmul_mx(
                        out=h_banks[t][:],
                        lhsT=w_q[0][:, cols].bitcast(FP8X4),
                        lhsT_scale=w_q[1][:, cols],
                        rhs=v_q[0][:].bitcast(FP8X4),
                        rhs_scale=v_q[1][:],
                        start=(step == 0),
                        stop=(step == 1),
                    )

        second_product(range(EARLY // P), 0, w1_early, w2_early)
        w1_late_woven = keep.tile([P, S - EARLY, PACK], BF16, name="w1_late_woven", tag="z2_woven", align_bytes=64)
        weave_into(nc.vector.tensor_copy, w1_late_woven[:], w1_raw[:, :, EARLY:])
        w2_late_woven = keep.tile([P, S - EARLY, PACK], BF16, name="w2_late_woven", tag="z2_planes", align_bytes=64)
        weave_into(nc.scalar.copy, w2_late_woven[:], w2_raw[:, :, EARLY:])
        w1_late = quantise(w1_late_woven, "w1_late")
        w2_late = quantise(w2_late_woven, "w2_late")
        second_product(range(EARLY // P, PACK), EARLY, w1_late, w2_late)

        def larger_of_h_and_smallest(piece):
            t, cols, result, smallest, largest = piece
            top = ring.tile([P, HALF], F32, name="top")
            nc.vector.tensor_tensor(top[:], h_rows[t][:, cols], smallest[:], ALU.max)
            return top

        def store(piece, top):
            t, cols, result, smallest, largest = piece
            nc.vector.scalar_tensor_tensor(result[:, cols], largest[:], -0.5, top[:], ALU.mult, ALU.add)
            nc.sync.dma_start(out[P * t : P * (t + 1), cols], result[:, cols])

        for t in range(1, PACK):
            nc.vector.tensor_copy(h_rows[t][:, :S], h_banks[t][:])
        nc.scalar.copy(h_rows[0][:, :S], h_banks[0][:])
        previous = None
        for t in range(PACK):
            result = ring.tile([P, S], F32, name="result")
            members = ring.tile([P, S, MEMBERS], F32, name="members")
            entries = members[:].rearrange("p j u -> p (j u)")
            for first in range(0, S * MEMBERS, GATHER):
                window = h_rows[t][:].indirect(n5_sb[:, first // LIST_ROWS : (first + GATHER) // LIST_ROWS])
                if t == 0 and first == GATHER:
                    nc.vector.tensor_copy(entries[:, first : first + GATHER], window)
                else:
                    nc.scalar.activation(entries[:, first : first + GATHER], window, ACT.Copy)
            for first in range(0, S, HALF):
                cols = slice(first, first + HALF)
                low = ring.tile([P, HALF, 2], F32, name="low")
                high = ring.tile([P, HALF, 2], F32, name="high")
                smallest = ring.tile([P, HALF], F32, name="smallest")
                largest = ring.tile([P, HALF], F32, name="largest")
                nc.vector.tensor_tensor(low[:], members[:, cols, 0:2], members[:, cols, 2:4], ALU.min)
                nc.vector.tensor_tensor(high[:], members[:, cols, 0:2], members[:, cols, 2:4], ALU.max)
                if previous is not None:
                    top = larger_of_h_and_smallest(previous)
                nc.vector.tensor_tensor(smallest[:], low[:, :, 0], low[:, :, 1], ALU.min)
                if previous is not None:
                    store(previous, top)
                nc.vector.tensor_tensor(largest[:], high[:, :, 0], high[:, :, 1], ALU.max)
                previous = (t, cols, result, smallest, largest)
        store(previous, larger_of_h_and_smallest(previous))
